import numpy as np
import ml_dtypes


def mxq(x, axis, fmt="e4m3"):
    dtype, down = {"e4m3": (ml_dtypes.float8_e4m3fn, 7), "e5m2": (ml_dtypes.float8_e5m2, 14)}[fmt]
    v = np.moveaxis(np.asarray(x, np.float32).astype(ml_dtypes.bfloat16).astype(np.float64), axis, -1)
    blocks = v.reshape(v.shape[:-1] + (-1, 32))
    amax = np.abs(blocks).max(-1, keepdims=True)
    byte = np.maximum(np.where(amax > 0, np.frexp(amax)[1] - 1 + 127, 0) - down, 1)
    scale = np.exp2(byte - 127.0)
    codes = (blocks / scale).astype(np.float32).astype(dtype).astype(np.float64)
    return np.moveaxis((codes * scale).reshape(v.shape), -1, axis)


WIDE = False


def mx_kscale(k):
    if not WIDE:
        return np.ones(k)
    levels = np.array([10, -10, 5, -5, 0])
    if k % 512:
        return np.exp2(np.random.permutation(np.resize(levels, k // 32))).repeat(32)
    a = np.empty((k // 512, 16))
    for p in range(k // 512):
        a[p, :8] = np.random.permutation(np.resize(levels, 8))
        for g in range(8):
            far = levels[np.abs(levels - a[p, g]) >= 10]
            a[p, g + 8] = far[np.random.randint(len(far))]
    return np.exp2(a.ravel()).repeat(32)


def f64(x):
    return np.asarray(x).astype(np.float64)


def striped8(idx):
    return np.concatenate([v.reshape(-1, 16).T for v in idx]).astype(np.uint16)


def unstriped8(offs):
    return np.stack([offs[16 * g:16 * g + 16].T.reshape(-1) for g in range(8)]).astype(np.int64)


E2M1 = np.array([0.0, 0.5, 1.0, 1.5, 2.0, 3.0, 4.0, 6.0, -0.0, -0.5, -1.0, -1.5, -2.0, -3.0, -4.0, -6.0])


def pack_weight(w, fmt):
    k, n = w.shape
    w = f64(np.asarray(w, np.float32).astype(ml_dtypes.bfloat16)).reshape(k // 32, 32, n)
    amax = np.abs(w).max(1)
    if fmt == "e4m3":
        byte = np.frexp(amax)[1] - 1 + 127 - 7
    else:
        mant, ex = np.frexp(amax / 6.0)
        byte = np.where(mant > 0.5, ex, ex - 1) + 127
    byte = np.clip(np.where(amax > 0, byte, 1), 1, 254)
    scaled = (w * np.exp2(127.0 - byte)[:, None, :]).reshape(k, n).astype(np.float32)
    by_word = np.ascontiguousarray(scaled.reshape(k // 512, 128, 4, n).transpose(0, 1, 3, 2))
    if fmt == "e4m3":
        words = by_word.astype(ml_dtypes.float8_e4m3fn).view(np.uint8)
    else:
        c = by_word.astype(ml_dtypes.float4_e2m1fn).view(np.uint8) & 0xF
        words = (c[..., 0::2] | (c[..., 1::2] << 4)).reshape(k // 512, 128, 2 * n)
    return np.ascontiguousarray(words), np.ascontiguousarray(byte.astype(np.uint8).reshape(k // 512, 16, n))


def unpack_weight(words, scales, fmt):
    g, _, n = scales.shape
    words = np.ascontiguousarray(words).reshape(g, 128, n, -1)
    if fmt == "e4m3":
        vals = words.view(ml_dtypes.float8_e4m3fn).astype(np.float64)
    else:
        nib = np.empty((g, 128, n, 4), np.uint8)
        nib[..., 0::2] = words & 0xF
        nib[..., 1::2] = words >> 4
        vals = E2M1[nib]
    vals = vals * np.repeat(np.exp2(scales.astype(np.float64) - 127.0), 8, axis=1)[..., None]
    return vals.transpose(0, 1, 3, 2).reshape(g * 512, n)


K, M, T, S = 512, 1024, 512, 256


def setup_inputs():
    n = np.random.standard_normal
    s = mx_kscale(K)[:, None]
    p_w = pack_weight(n((K, M)) / np.sqrt(K) / s, "e4m3")
    return {
        "x": (n((K, S)) * s).astype(np.float32),
        "w_words": p_w[0],
        "w_scales": p_w[1],
        "b": (0.3 * n(1024)).astype(np.float32),
        "wgo": np.repeat(np.random.uniform(0.5, 2.0, (8, S)), 16, axis=0).astype(np.float32),
        "offs": striped8(np.stack([np.random.permutation(T)[:S] for _ in range(8)])),
    }


def reference(x, w_words, w_scales, b, wgo, offs):
    x_ = mxq(f64(x), 0, "e4m3")
    w_ = unpack_weight(w_words, w_scales, "e4m3")
    y = w_.T @ x_
    place = unstriped8(offs)[np.arange(M) % 128 // 16]
    out = np.zeros((M, T))
    out[np.arange(M)[:, None], place] = f64(wgo)[np.arange(M) % 128] * (y + f64(b)[:, None])
    return out

@@ -1,0 +1,124 @@
+from contextlib import ExitStack
+
+import concourse.mybir as mybir
+from concourse.masks import make_identity
+
+K, M, T, S = 512, 1024, 512, 256
+FLOPS = 2 * K * M * S
+
+P = 128
+BLOCKS = M // P
+HALF = 128
+F32 = mybir.dt.float32
+BF16 = mybir.dt.bfloat16
+I32 = mybir.dt.int32
+U32 = mybir.dt.uint32
+U16 = mybir.dt.uint16
+U8 = mybir.dt.uint8
+FP8X4 = mybir.dt.float8_e4m3fn_x4
+MULT = mybir.AluOpType.mult
+IDENTITY = mybir.ActivationFunctionType.Identity
+
+
+def tile_list_hscat_bias_kernel(tc, x, w_words, w_scales, b, wgo, offs, out):
+    nc = tc.nc
+    with ExitStack() as ctx:
+        keep = ctx.enter_context(tc.tile_pool(name="keep", bufs=1))
+        wpool = ctx.enter_context(tc.tile_pool(name="wpool", bufs=6))
+        ypool = ctx.enter_context(tc.tile_pool(name="ypool", bufs=6))
+        psum = ctx.enter_context(tc.psum_pool(name="psum", bufs=6))
+        bpsum = ctx.enter_context(tc.psum_pool(name="bpsum", bufs=1))
+
+        offsets = keep.tile([P, S // 16], U16, name="offsets")
+
+        xv = x.rearrange("(p j) w -> p j w", j=4)
+        raw = keep.tile([P, 4, S], F32, name="raw")
+        w_bytes = w_words[0].rearrange("p n t -> p (n t)")
+        w_codes = keep.tile([P, M], U32, name="w_codes", align_bytes=64)
+        w_sc = keep.tile([P, M], U8, name="w_sc", align_bytes=64)
+        wgo_sb = keep.tile([P, S], F32, name="wgo_sb")
+        b_rows = keep.tile([P, P], F32, name="b_rows")
+        bias = keep.tile([P, BLOCKS], F32, name="bias")
+        ident = keep.tile([P, P], F32, name="ident")
+        warm = keep.tile([P, 1], F32, name="warm")
+
+        nc.gpsimd.memset(b_rows[:], 0.0)
+        nc.gpsimd.memset(warm[:], 0.0)
+        nc.sync.dma_start(offsets[:], offs)
+        nc.sync.dma_start(raw[:], xv)
+        nc.sync.dma_start(b_rows[0:BLOCKS, :], b.rearrange("(c p) -> c p", p=P))
+        for q in range(4):
+            nc.scalar.dma_start(
+                w_sc[32 * q : 32 * q + 4, :].bitcast(I32), w_scales[0][4 * q : 4 * q + 4, :].bitcast(I32)
+            )
+        nc.scalar.dma_start(w_codes[:].bitcast(I32), w_bytes.bitcast(I32))
+        nc.gpsimd.dma_start(wgo_sb[:], wgo)
+        make_identity(nc, ident[:])
+        nc.scalar.activation(warm[:], warm[:], IDENTITY, bias=warm[:])
+
+        windows = {}
+
+        def clear(c, engine):
+            windows[c] = wpool.tile([P, T], F32, name="window")
+            engine.memset(windows[c][:], 0.0)
+
+        for c in range(4):
+            clear(c, nc.vector)
+        for c in (4, 5):
+            clear(c, nc.gpsimd)
+
+        b_turned = bpsum.tile([P, P], F32, name="b_turned")
+        nc.tensor.transpose(b_turned[:], b_rows[:], ident[:])
+        nc.scalar.copy(bias[:], b_turned[:, 0:BLOCKS])
+
+        codes = [keep.tile([P, HALF], U32, name=f"codes{h}", align_bytes=64) for h in range(2)]
+        scales = [keep.tile([P, HALF], U8, name=f"scales{h}", align_bytes=64) for h in range(2)]
+        grouped = [keep.tile([P, HALF, 4], BF16, name=f"grouped{h}", align_bytes=64) for h in range(2)]
+
+        def cast(h, engine_copy):
+            engine_copy(
+                grouped[h][:].rearrange("p (c i) t -> p c t i", i=4),
+                raw[:, :, HALF * h : HALF * (h + 1)].rearrange("p t (c i) -> p c t i", i=4),
+            )
+
+        def quantize(h):
+            nc.vector.quantize_mx(
+                out=codes[h][:].bitcast(FP8X4),
+                scales=scales[h][:],
+                in_=grouped[h][:].rearrange("p w t -> p (w t)"),
+            )
+
+        def product(c, h):
+            acc = psum.tile([P, HALF], F32, name="acc")
+            nc.tensor.matmul_mx(
+                out=acc[:],
+                lhsT=w_codes[:, P * c : P * (c + 1)].bitcast(FP8X4),
+                lhsT_scale=w_sc[:, P * c : P * (c + 1)],
+                rhs=codes[h][:].bitcast(FP8X4),
+                rhs_scale=scales[h][:],
+                start=True,
+                stop=True,
+            )
+            y = ypool.tile([P, HALF], F32, name="y")
+            nc.scalar.activation(y[:], acc[:], IDENTITY, bias=bias[:, c : c + 1])
+            return y
+
+        def place(c, h):
+            y = product(c, h)
+            nc.vector.tensor_tensor(
+                windows[c][:].indirect(offsets[:, 8 * h : 8 * h + 8]), y[:], wgo_sb[:, HALF * h : HALF * (h + 1)], MULT
+            )
+            if h == 1:
+                nc.sync.dma_start(out[P * c : P * (c + 1), :], windows[c][:])
+
+        cast(0, nc.vector.tensor_copy)
+        cast(1, nc.scalar.copy)
+        quantize(0)
+        quantize(1)
+        for pair in range(0, BLOCKS, 2):
+            if pair == 6:
+                clear(6, nc.gpsimd)
+                clear(7, nc.gpsimd)
+            for h in range(2):
+                for c in (pair, pair + 1):
+                    place(c, h)

@@ -1,7 +1,7 @@
 from contextlib import ExitStack
 
 import concourse.mybir as mybir
-from concourse.masks import make_identity
+
 
 K, M, T, S = 512, 1024, 512, 256
 FLOPS = 2 * K * M * S
@@ -24,101 +24,94 @@ def tile_list_hscat_bias_kernel(tc, x, w_words, w_scales, b, wgo, offs, out):
     nc = tc.nc
     with ExitStack() as ctx:
         keep = ctx.enter_context(tc.tile_pool(name="keep", bufs=1))
-        wpool = ctx.enter_context(tc.tile_pool(name="wpool", bufs=6))
         ypool = ctx.enter_context(tc.tile_pool(name="ypool", bufs=6))
         psum = ctx.enter_context(tc.psum_pool(name="psum", bufs=6))
-        bpsum = ctx.enter_context(tc.psum_pool(name="bpsum", bufs=1))
 
         offsets = keep.tile([P, S // 16], U16, name="offsets")
 
         xv = x.rearrange("(p j) w -> p j w", j=4)
-        raw = keep.tile([P, 4, S], F32, name="raw")
+        raw = [keep.tile([P, 4, HALF], F32, name=f"raw{h}") for h in range(2)]
         w_bytes = w_words[0].rearrange("p n t -> p (n t)")
-        w_codes = keep.tile([P, M], U32, name="w_codes", align_bytes=64)
+        FIRST = 2 * P
+        w_first = keep.tile([P, FIRST], U32, name="w_first", align_bytes=64)
+        w_rest = keep.tile([P, M - FIRST], U32, name="w_rest", align_bytes=64)
         w_sc = keep.tile([P, M], U8, name="w_sc", align_bytes=64)
         wgo_sb = keep.tile([P, S], F32, name="wgo_sb")
-        b_rows = keep.tile([P, P], F32, name="b_rows")
-        bias = keep.tile([P, BLOCKS], F32, name="bias")
-        ident = keep.tile([P, P], F32, name="ident")
+        b_rows = keep.tile([P, 32], F32, name="b_rows", align_bytes=64)
+        bias = keep.tile([P, 32], F32, name="bias", align_bytes=64)
         warm = keep.tile([P, 1], F32, name="warm")
 
-        nc.gpsimd.memset(b_rows[:], 0.0)
-        nc.gpsimd.memset(warm[:], 0.0)
-        nc.sync.dma_start(offsets[:], offs)
-        nc.sync.dma_start(raw[:], xv)
-        nc.sync.dma_start(b_rows[0:BLOCKS, :], b.rearrange("(c p) -> c p", p=P))
-        for q in range(4):
-            nc.scalar.dma_start(
+        def load_scales(q, engine):
+            engine.dma_start(
                 w_sc[32 * q : 32 * q + 4, :].bitcast(I32), w_scales[0][4 * q : 4 * q + 4, :].bitcast(I32)
             )
-        nc.scalar.dma_start(w_codes[:].bitcast(I32), w_bytes.bitcast(I32))
-        nc.gpsimd.dma_start(wgo_sb[:], wgo)
-        make_identity(nc, ident[:])
+
+        nc.gpsimd.memset(b_rows[:], 0.0)
+        nc.vector.memset(warm[:], 0.0)
+        load_scales(0, nc.sync)
+        nc.scalar.dma_start(b_rows[0:P:4, :], b.rearrange("(c q i) -> q c i", q=4, i=32))
+        load_scales(1, nc.scalar)
+        nc.sync.dma_start(raw[0][:], xv[:, :, 0:HALF])
+        load_scales(2, nc.scalar)
+        load_scales(3, nc.scalar)
+        nc.sync.dma_start(w_first[:].bitcast(I32), w_bytes[:, 0 : 4 * FIRST].bitcast(I32))
+        nc.sync.dma_start(raw[1][:], xv[:, :, HALF:S])
+        nc.sync.dma_start(offsets[:], offs)
+        nc.sync.dma_start(wgo_sb[:], wgo)
+        nc.sync.dma_start(w_rest[:].bitcast(I32), w_bytes[:, 4 * FIRST :].bitcast(I32))
         nc.scalar.activation(warm[:], warm[:], IDENTITY, bias=warm[:])
 
-        windows = {}
+        windows = [keep.tile([P, T], F32, name=f"window{i}") for i in range(4)]
+        for window in windows:
+            nc.vector.memset(window[:], 0.0)
 
-        def clear(c, engine):
-            windows[c] = wpool.tile([P, T], F32, name="window")
-            engine.memset(windows[c][:], 0.0)
+        nc.vector.transpose(bias[:], b_rows[:])
 
-        for c in range(4):
-            clear(c, nc.vector)
-        for c in (4, 5):
-            clear(c, nc.gpsimd)
-
-        b_turned = bpsum.tile([P, P], F32, name="b_turned")
-        nc.tensor.transpose(b_turned[:], b_rows[:], ident[:])
-        nc.scalar.copy(bias[:], b_turned[:, 0:BLOCKS])
-
-        codes = [keep.tile([P, HALF], U32, name=f"codes{h}", align_bytes=64) for h in range(2)]
-        scales = [keep.tile([P, HALF], U8, name=f"scales{h}", align_bytes=64) for h in range(2)]
+        codes = keep.tile([P, S], U32, name="codes", align_bytes=64)
+        scales = keep.tile([P, S], U8, name="scales", align_bytes=64)
         grouped = [keep.tile([P, HALF, 4], BF16, name=f"grouped{h}", align_bytes=64) for h in range(2)]
 
         def cast(h, engine_copy):
             engine_copy(
                 grouped[h][:].rearrange("p (c i) t -> p c t i", i=4),
-                raw[:, :, HALF * h : HALF * (h + 1)].rearrange("p t (c i) -> p c t i", i=4),
+                raw[h][:].rearrange("p t (c i) -> p c t i", i=4),
             )
 
         def quantize(h):
             nc.vector.quantize_mx(
-                out=codes[h][:].bitcast(FP8X4),
-                scales=scales[h][:],
+                out=codes[:, HALF * h : HALF * (h + 1)].bitcast(FP8X4),
+                scales=scales[:, HALF * h : HALF * (h + 1)],
                 in_=grouped[h][:].rearrange("p w t -> p (w t)"),
             )
 
-        def product(c, h):
-            acc = psum.tile([P, HALF], F32, name="acc")
+        def place(c, lo, hi):
+            acc = psum.tile([P, S], F32, name="acc")
+            n = P * c
+            w_codes = w_first[:, n : n + P] if n < FIRST else w_rest[:, n - FIRST : n - FIRST + P]
             nc.tensor.matmul_mx(
-                out=acc[:],
-                lhsT=w_codes[:, P * c : P * (c + 1)].bitcast(FP8X4),
-                lhsT_scale=w_sc[:, P * c : P * (c + 1)],
-                rhs=codes[h][:].bitcast(FP8X4),
-                rhs_scale=scales[h][:],
+                out=acc[:, lo:hi],
+                lhsT=w_codes.bitcast(FP8X4),
+                lhsT_scale=w_sc[:, n : n + P],
+                rhs=codes[:, lo:hi].bitcast(FP8X4),
+                rhs_scale=scales[:, lo:hi],
                 start=True,
                 stop=True,
             )
-            y = ypool.tile([P, HALF], F32, name="y")
-            nc.scalar.activation(y[:], acc[:], IDENTITY, bias=bias[:, c : c + 1])
-            return y
-
-        def place(c, h):
-            y = product(c, h)
+            y = ypool.tile([P, S], F32, name="y")
+            nc.scalar.activation(y[:, lo:hi], acc[:, lo:hi], IDENTITY, bias=bias[:, 4 * c : 4 * c + 1])
+            window = windows[c % len(windows)]
             nc.vector.tensor_tensor(
-                windows[c][:].indirect(offsets[:, 8 * h : 8 * h + 8]), y[:], wgo_sb[:, HALF * h : HALF * (h + 1)], MULT
+                window[:].indirect(offsets[:, lo // 16 : hi // 16]), y[:, lo:hi], wgo_sb[:, lo:hi], MULT
             )
-            if h == 1:
-                nc.sync.dma_start(out[P * c : P * (c + 1), :], windows[c][:])
+            if hi == S:
+                nc.sync.dma_start(out[n : n + P, :], window[:])
 
         cast(0, nc.vector.tensor_copy)
-        cast(1, nc.scalar.copy)
         quantize(0)
+        cast(1, nc.vector.tensor_copy)
         quantize(1)
-        for pair in range(0, BLOCKS, 2):
-            if pair == 6:
-                clear(6, nc.gpsimd)
-                clear(7, nc.gpsimd)
-            for h in range(2):
-                for c in (pair, pair + 1):
-                    place(c, h)
+        for h in range(2):
+            for c in range(2):
+                place(c, HALF * h, HALF * (h + 1))
+        for c in range(2, BLOCKS):
+            place(c, 0, S)

@@ -49,15 +49,15 @@ def tile_list_hscat_bias_kernel(tc, x, w_words, w_scales, b, wgo, offs, out):
         nc.gpsimd.memset(b_rows[:], 0.0)
         nc.vector.memset(warm[:], 0.0)
         load_scales(0, nc.sync)
-        nc.scalar.dma_start(b_rows[0:P:4, :], b.rearrange("(c q i) -> q c i", q=4, i=32))
         load_scales(1, nc.scalar)
-        nc.sync.dma_start(raw[0][:], xv[:, :, 0:HALF])
         load_scales(2, nc.scalar)
+        nc.sync.dma_start(raw[0][:], xv[:, :, 0:HALF])
         load_scales(3, nc.scalar)
+        nc.scalar.dma_start(b_rows[0:P:4, :], b.rearrange("(c q i) -> q c i", q=4, i=32))
         nc.sync.dma_start(w_first[:].bitcast(I32), w_bytes[:, 0 : 4 * FIRST].bitcast(I32))
         nc.sync.dma_start(raw[1][:], xv[:, :, HALF:S])
-        nc.sync.dma_start(offsets[:], offs)
         nc.sync.dma_start(wgo_sb[:], wgo)
+        nc.sync.dma_start(offsets[:], offs)
         nc.sync.dma_start(w_rest[:].bitcast(I32), w_bytes[:, 4 * FIRST :].bitcast(I32))
         nc.scalar.activation(warm[:], warm[:], IDENTITY, bias=warm[:])
 
@@ -71,17 +71,17 @@ def tile_list_hscat_bias_kernel(tc, x, w_words, w_scales, b, wgo, offs, out):
         scales = keep.tile([P, S], U8, name="scales", align_bytes=64)
         grouped = [keep.tile([P, HALF, 4], BF16, name=f"grouped{h}", align_bytes=64) for h in range(2)]
 
-        def cast(h, engine_copy):
+        def cast(h, lo, hi, engine_copy):
             engine_copy(
-                grouped[h][:].rearrange("p (c i) t -> p c t i", i=4),
-                raw[h][:].rearrange("p t (c i) -> p c t i", i=4),
+                grouped[h][:, lo:hi, :].rearrange("p (c i) t -> p c t i", i=4),
+                raw[h][:, :, lo:hi].rearrange("p t (c i) -> p c t i", i=4),
             )
 
-        def quantize(h):
+        def quantize(h, lo, hi):
             nc.vector.quantize_mx(
-                out=codes[:, HALF * h : HALF * (h + 1)].bitcast(FP8X4),
-                scales=scales[:, HALF * h : HALF * (h + 1)],
-                in_=grouped[h][:].rearrange("p w t -> p (w t)"),
+                out=codes[:, HALF * h + lo : HALF * h + hi].bitcast(FP8X4),
+                scales=scales[:, HALF * h + lo : HALF * h + hi],
+                in_=grouped[h][:, lo:hi, :].rearrange("p w t -> p (w t)"),
             )
 
         def place(c, lo, hi):
@@ -106,10 +106,11 @@ def tile_list_hscat_bias_kernel(tc, x, w_words, w_scales, b, wgo, offs, out):
             if hi == S:
                 nc.sync.dma_start(out[n : n + P, :], window[:])
 
-        cast(0, nc.vector.tensor_copy)
-        quantize(0)
-        cast(1, nc.vector.tensor_copy)
-        quantize(1)
+        for h in range(2):
+            cast(h, 0, 64, nc.vector.tensor_copy)
+            cast(h, 64, 128, nc.scalar.copy if h else nc.vector.tensor_copy)
+            quantize(h, 0, 64)
+            quantize(h, 64, 128)
         for h in range(2):
             for c in range(2):
                 place(c, HALF * h, HALF * (h + 1))

@@ -39,7 +39,6 @@ def tile_list_hscat_bias_kernel(tc, x, w_words, w_scales, b, wgo, offs, out):
         wgo_sb = keep.tile([P, S], F32, name="wgo_sb")
         b_rows = keep.tile([P, 32], F32, name="b_rows", align_bytes=64)
         bias = keep.tile([P, 32], F32, name="bias", align_bytes=64)
-        warm = keep.tile([P, 1], F32, name="warm")
 
         def load_scales(q, engine):
             engine.dma_start(
@@ -47,19 +46,17 @@ def tile_list_hscat_bias_kernel(tc, x, w_words, w_scales, b, wgo, offs, out):
             )
 
         nc.gpsimd.memset(b_rows[:], 0.0)
-        nc.vector.memset(warm[:], 0.0)
         load_scales(0, nc.sync)
         load_scales(1, nc.scalar)
         load_scales(2, nc.scalar)
         nc.sync.dma_start(raw[0][:], xv[:, :, 0:HALF])
         load_scales(3, nc.scalar)
-        nc.scalar.dma_start(b_rows[0:P:4, :], b.rearrange("(c q i) -> q c i", q=4, i=32))
+        nc.sync.dma_start(b_rows[0:P:4, :], b.rearrange("(c q i) -> q c i", q=4, i=32))
         nc.sync.dma_start(w_first[:].bitcast(I32), w_bytes[:, 0 : 4 * FIRST].bitcast(I32))
-        nc.sync.dma_start(raw[1][:], xv[:, :, HALF:S])
+        nc.scalar.dma_start(raw[1][:], xv[:, :, HALF:S])
         nc.sync.dma_start(wgo_sb[:], wgo)
         nc.sync.dma_start(offsets[:], offs)
         nc.sync.dma_start(w_rest[:].bitcast(I32), w_bytes[:, 4 * FIRST :].bitcast(I32))
-        nc.scalar.activation(warm[:], warm[:], IDENTITY, bias=warm[:])
 
         windows = [keep.tile([P, T], F32, name=f"window{i}") for i in range(4)]
         for window in windows:

@@ -54,8 +54,9 @@ def tile_list_hscat_bias_kernel(tc, x, w_words, w_scales, b, wgo, offs, out):
         nc.sync.dma_start(b_rows[0:P:4, :], b.rearrange("(c q i) -> q c i", q=4, i=32))
         nc.sync.dma_start(w_first[:].bitcast(I32), w_bytes[:, 0 : 4 * FIRST].bitcast(I32))
         nc.scalar.dma_start(raw[1][:], xv[:, :, HALF:S])
-        nc.sync.dma_start(wgo_sb[:], wgo)
         nc.sync.dma_start(offsets[:], offs)
+        nc.sync.dma_start(wgo_sb[:, 0:HALF], wgo[:, 0:HALF])
+        nc.sync.dma_start(wgo_sb[:, HALF:S], wgo[:, HALF:S])
         nc.sync.dma_start(w_rest[:].bitcast(I32), w_bytes[:, 4 * FIRST :].bitcast(I32))
 
         windows = [keep.tile([P, T], F32, name=f"window{i}") for i in range(4)]

@@ -35,14 +35,15 @@ def tile_list_hscat_bias_kernel(tc, x, w_words, w_scales, b, wgo, offs, out):
         FIRST = 2 * P
         w_first = keep.tile([P, FIRST], U32, name="w_first", align_bytes=64)
         w_rest = keep.tile([P, M - FIRST], U32, name="w_rest", align_bytes=64)
-        w_sc = keep.tile([P, M], U8, name="w_sc", align_bytes=64)
+        w_sc = keep.tile([P, M // 4], U8, name="w_sc", align_bytes=64)
         wgo_sb = keep.tile([P, S], F32, name="wgo_sb")
         b_rows = keep.tile([P, 32], F32, name="b_rows", align_bytes=64)
         bias = keep.tile([P, 32], F32, name="bias", align_bytes=64)
 
         def load_scales(q, engine):
             engine.dma_start(
-                w_sc[32 * q : 32 * q + 4, :].bitcast(I32), w_scales[0][4 * q : 4 * q + 4, :].bitcast(I32)
+                w_sc[32 * q : 32 * q + 16, :].bitcast(I32),
+                w_scales[0][4 * q : 4 * q + 4, :].rearrange("r (a n) -> a r n", a=4).bitcast(I32),
             )
 
         nc.gpsimd.memset(b_rows[:], 0.0)
@@ -89,7 +90,7 @@ def tile_list_hscat_bias_kernel(tc, x, w_words, w_scales, b, wgo, offs, out):
             nc.tensor.matmul_mx(
                 out=acc[:, lo:hi],
                 lhsT=w_codes.bitcast(FP8X4),
-                lhsT_scale=w_sc[:, n : n + P],
+                lhsT_scale=w_sc[4 * (c // 2) :, P * (c % 2) : P * (c % 2 + 1)],
                 rhs=codes[:, lo:hi].bitcast(FP8X4),
                 rhs_scale=scales[:, lo:hi],
                 start=True,

@@ -34,7 +34,7 @@ def tile_list_hscat_bias_kernel(tc, x, w_words, w_scales, b, wgo, offs, out):
         w_bytes = w_words[0].rearrange("p n t -> p (n t)")
         FIRST = 2 * P
         w_first = keep.tile([P, FIRST], U32, name="w_first", align_bytes=64)
-        w_rest = keep.tile([P, M - FIRST], U32, name="w_rest", align_bytes=64)
+        w_rest = [keep.tile([P, 3 * P], U32, name=f"w_rest{i}", align_bytes=64) for i in range(2)]
         w_sc = keep.tile([P, M // 4], U8, name="w_sc", align_bytes=64)
         wgo_sb = keep.tile([P, S], F32, name="wgo_sb")
         b_rows = keep.tile([P, 32], F32, name="b_rows", align_bytes=64)
@@ -58,7 +58,9 @@ def tile_list_hscat_bias_kernel(tc, x, w_words, w_scales, b, wgo, offs, out):
         nc.sync.dma_start(offsets[:], offs)
         nc.sync.dma_start(wgo_sb[:, 0:HALF], wgo[:, 0:HALF])
         nc.sync.dma_start(wgo_sb[:, HALF:S], wgo[:, HALF:S])
-        nc.sync.dma_start(w_rest[:].bitcast(I32), w_bytes[:, 4 * FIRST :].bitcast(I32))
+        for i in range(2):
+            lo = 4 * (FIRST + 3 * P * i)
+            nc.sync.dma_start(w_rest[i][:].bitcast(I32), w_bytes[:, lo : lo + 12 * P].bitcast(I32))
 
         windows = [keep.tile([P, T], F32, name=f"window{i}") for i in range(4)]
         for window in windows:
@@ -86,7 +88,7 @@ def tile_list_hscat_bias_kernel(tc, x, w_words, w_scales, b, wgo, offs, out):
         def place(c, lo, hi):
             acc = psum.tile([P, S], F32, name="acc")
             n = P * c
-            w_codes = w_first[:, n : n + P] if n < FIRST else w_rest[:, n - FIRST : n - FIRST + P]
+            w_codes = w_first[:, n : n + P] if n < FIRST else w_rest[(c - 2) // 3][:, P * ((c - 2) % 3) : P * ((c - 2) % 3 + 1)]
             nc.tensor.matmul_mx(
                 out=acc[:, lo:hi],
                 lhsT=w_codes.bitcast(FP8X4),
@@ -103,7 +105,11 @@ def tile_list_hscat_bias_kernel(tc, x, w_words, w_scales, b, wgo, offs, out):
                 window[:].indirect(offsets[:, lo // 16 : hi // 16]), y[:, lo:hi], wgo_sb[:, lo:hi], MULT
             )
             if hi == S:
-                nc.sync.dma_start(out[n : n + P, :], window[:])
+                if 4 <= c < BLOCKS - 1:
+                    nc.sync.dma_start(out[n : n + P, 0 : T // 2], window[:, 0 : T // 2])
+                    nc.sync.dma_start(out[n : n + P, T // 2 : T], window[:, T // 2 : T])
+                else:
+                    nc.sync.dma_start(out[n : n + P, :], window[:])
 
         for h in range(2):
             cast(h, 0, 64, nc.vector.tensor_copy)

@@ -9,6 +9,10 @@ FLOPS = 2 * K * M * S
 P = 128
 BLOCKS = M // P
 HALF = 128
+PIECE = 64
+SPLIT = 5
+WINDOWS = 5
+W_CUTS = (0, 3, 5, 8)
 F32 = mybir.dt.float32
 BF16 = mybir.dt.bfloat16
 I32 = mybir.dt.int32
@@ -24,21 +28,25 @@ def tile_list_hscat_bias_kernel(tc, x, w_words, w_scales, b, wgo, offs, out):
     nc = tc.nc
     with ExitStack() as ctx:
         keep = ctx.enter_context(tc.tile_pool(name="keep", bufs=1))
-        ypool = ctx.enter_context(tc.tile_pool(name="ypool", bufs=6))
-        psum = ctx.enter_context(tc.psum_pool(name="psum", bufs=6))
+        turn = ctx.enter_context(tc.tile_pool(name="turn", bufs=1))
+        ypool = ctx.enter_context(tc.tile_pool(name="ypool", bufs=8))
+        psum = ctx.enter_context(tc.psum_pool(name="psum", bufs=8))
 
         offsets = keep.tile([P, S // 16], U16, name="offsets")
-
         xv = x.rearrange("(p j) w -> p j w", j=4)
-        raw = [keep.tile([P, 4, HALF], F32, name=f"raw{h}") for h in range(2)]
+        raw = [
+            keep.tile([P, 4, HALF], F32, name="raw0"),
+            turn.tile([P, 4, HALF], F32, name="raw1", align_bytes=64, offset=2048),
+        ]
         w_bytes = w_words[0].rearrange("p n t -> p (n t)")
-        FIRST = 2 * P
-        w_first = keep.tile([P, FIRST], U32, name="w_first", align_bytes=64)
-        w_rest = [keep.tile([P, 3 * P], U32, name=f"w_rest{i}", align_bytes=64) for i in range(2)]
+        w_parts = [
+            keep.tile([P, P * (W_CUTS[i + 1] - W_CUTS[i])], U32, name=f"w_part{i}", align_bytes=64)
+            for i in range(len(W_CUTS) - 1)
+        ]
         w_sc = keep.tile([P, M // 4], U8, name="w_sc", align_bytes=64)
         wgo_sb = keep.tile([P, S], F32, name="wgo_sb")
         b_rows = keep.tile([P, 32], F32, name="b_rows", align_bytes=64)
-        bias = keep.tile([P, 32], F32, name="bias", align_bytes=64)
+        windows = [keep.tile([P, T], F32, name=f"window{i}") for i in range(WINDOWS)]
 
         def load_scales(q, engine):
             engine.dma_start(
@@ -46,64 +54,80 @@ def tile_list_hscat_bias_kernel(tc, x, w_words, w_scales, b, wgo, offs, out):
                 w_scales[0][4 * q : 4 * q + 4, :].rearrange("r (a n) -> a r n", a=4).bitcast(I32),
             )
 
+        def load_x(h, engine):
+            engine.dma_start(raw[h][:], xv[:, :, HALF * h : HALF * (h + 1)])
+
+        def load_w(i, engine):
+            lo, hi = 4 * P * W_CUTS[i], 4 * P * W_CUTS[i + 1]
+            engine.dma_start(w_parts[i][:].bitcast(I32), w_bytes[:, lo:hi].bitcast(I32))
+
+        def load_wgo(h, engine):
+            engine.dma_start(wgo_sb[:, HALF * h : HALF * (h + 1)], wgo[:, HALF * h : HALF * (h + 1)])
+
+        def load_b(engine):
+            engine.dma_start(b_rows[0:P:4, :], b.rearrange("(c q i) -> q c i", q=4, i=32))
+
         nc.gpsimd.memset(b_rows[:], 0.0)
         load_scales(0, nc.sync)
-        load_scales(1, nc.scalar)
-        load_scales(2, nc.scalar)
-        nc.sync.dma_start(raw[0][:], xv[:, :, 0:HALF])
-        load_scales(3, nc.scalar)
-        nc.sync.dma_start(b_rows[0:P:4, :], b.rearrange("(c q i) -> q c i", q=4, i=32))
-        nc.sync.dma_start(w_first[:].bitcast(I32), w_bytes[:, 0 : 4 * FIRST].bitcast(I32))
-        nc.scalar.dma_start(raw[1][:], xv[:, :, HALF:S])
+        load_x(0, nc.scalar)
+        load_scales(1, nc.sync)
+        load_w(0, nc.scalar)
+        load_scales(2, nc.sync)
+        load_wgo(0, nc.scalar)
+        load_scales(3, nc.sync)
+        load_b(nc.sync)
         nc.sync.dma_start(offsets[:], offs)
-        nc.sync.dma_start(wgo_sb[:, 0:HALF], wgo[:, 0:HALF])
-        nc.sync.dma_start(wgo_sb[:, HALF:S], wgo[:, HALF:S])
-        for i in range(2):
-            lo = 4 * (FIRST + 3 * P * i)
-            nc.sync.dma_start(w_rest[i][:].bitcast(I32), w_bytes[:, lo : lo + 12 * P].bitcast(I32))
+        load_x(1, nc.sync)
+        load_w(1, nc.sync)
+        load_wgo(1, nc.sync)
+        load_w(2, nc.sync)
 
-        windows = [keep.tile([P, T], F32, name=f"window{i}") for i in range(4)]
-        for window in windows:
+        for window in windows[0:4]:
             nc.vector.memset(window[:], 0.0)
-
-        nc.vector.transpose(bias[:], b_rows[:])
+        for window in windows[4:]:
+            nc.gpsimd.memset(window[:], 0.0)
 
         codes = keep.tile([P, S], U32, name="codes", align_bytes=64)
         scales = keep.tile([P, S], U8, name="scales", align_bytes=64)
-        grouped = [keep.tile([P, HALF, 4], BF16, name=f"grouped{h}", align_bytes=64) for h in range(2)]
 
-        def cast(h, lo, hi, engine_copy):
+        def cast(piece, h, base, lo, hi, engine_copy):
             engine_copy(
-                grouped[h][:, lo:hi, :].rearrange("p (c i) t -> p c t i", i=4),
-                raw[h][:, :, lo:hi].rearrange("p t (c i) -> p c t i", i=4),
+                piece[:, lo:hi, :].rearrange("p (c i) t -> p c t i", i=4),
+                raw[h][:, :, base + lo : base + hi].rearrange("p t (c i) -> p c t i", i=4),
             )
 
-        def quantize(h, lo, hi):
+        def quantize(piece, lo, hi):
             nc.vector.quantize_mx(
-                out=codes[:, HALF * h + lo : HALF * h + hi].bitcast(FP8X4),
-                scales=scales[:, HALF * h + lo : HALF * h + hi],
-                in_=grouped[h][:, lo:hi, :].rearrange("p w t -> p (w t)"),
+                out=codes[:, lo:hi].bitcast(FP8X4),
+                scales=scales[:, lo:hi],
+                in_=piece[:].rearrange("p w t -> p (w t)"),
             )
 
-        def place(c, lo, hi):
-            acc = psum.tile([P, S], F32, name="acc")
-            n = P * c
-            w_codes = w_first[:, n : n + P] if n < FIRST else w_rest[(c - 2) // 3][:, P * ((c - 2) % 3) : P * ((c - 2) % 3 + 1)]
+        def multiply(c, acc, lo, hi):
+            i = max(k for k in range(len(W_CUTS) - 1) if W_CUTS[k] <= c)
+            first = P * (c - W_CUTS[i])
             nc.tensor.matmul_mx(
-                out=acc[:, lo:hi],
-                lhsT=w_codes.bitcast(FP8X4),
+                out=acc,
+                lhsT=w_parts[i][:, first : first + P].bitcast(FP8X4),
                 lhsT_scale=w_sc[4 * (c // 2) :, P * (c % 2) : P * (c % 2 + 1)],
                 rhs=codes[:, lo:hi].bitcast(FP8X4),
                 rhs_scale=scales[:, lo:hi],
                 start=True,
                 stop=True,
             )
-            y = ypool.tile([P, S], F32, name="y")
-            nc.scalar.activation(y[:, lo:hi], acc[:, lo:hi], IDENTITY, bias=bias[:, 4 * c : 4 * c + 1])
-            window = windows[c % len(windows)]
-            nc.vector.tensor_tensor(
-                window[:].indirect(offsets[:, lo // 16 : hi // 16]), y[:, lo:hi], wgo_sb[:, lo:hi], MULT
-            )
+
+        def place(c, lo, hi, y=None):
+            acc = psum.tile([P, hi - lo], F32, name="acc")
+            multiply(c, acc[:], lo, hi)
+            if y is None:
+                y = ypool.tile([P, hi - lo], F32, name="y")
+            nc.scalar.activation(y[:], acc[:], IDENTITY, bias=bias[:, 4 * c : 4 * c + 1])
+            scatter(c, lo, hi, y)
+
+        def scatter(c, lo, hi, y):
+            n = P * c
+            window = windows[c % WINDOWS]
+            nc.vector.tensor_tensor(window[:].indirect(offsets[:, lo // 16 : hi // 16]), y[:], wgo_sb[:, lo:hi], MULT)
             if hi == S:
                 if 4 <= c < BLOCKS - 1:
                     nc.sync.dma_start(out[n : n + P, 0 : T // 2], window[:, 0 : T // 2])
@@ -111,13 +135,30 @@ def tile_list_hscat_bias_kernel(tc, x, w_words, w_scales, b, wgo, offs, out):
                 else:
                     nc.sync.dma_start(out[n : n + P, :], window[:])
 
-        for h in range(2):
-            cast(h, 0, 64, nc.vector.tensor_copy)
-            cast(h, 64, 128, nc.scalar.copy if h else nc.vector.tensor_copy)
-            quantize(h, 0, 64)
-            quantize(h, 64, 128)
-        for h in range(2):
-            for c in range(2):
-                place(c, HALF * h, HALF * (h + 1))
-        for c in range(2, BLOCKS):
+        piece0 = keep.tile([P, PIECE, 4], BF16, name="piece0", align_bytes=64)
+        piece1 = turn.tile([P, PIECE, 4], BF16, name="piece1", align_bytes=64, offset=0)
+        cast(piece0, 0, 0, 0, PIECE, nc.vector.tensor_copy)
+        cast(piece1, 0, PIECE, 0, 32, nc.vector.tensor_copy)
+        cast(piece1, 0, PIECE, 32, PIECE, nc.scalar.copy)
+        quantize(piece0, 0, PIECE)
+        quantize(piece1, PIECE, HALF)
+        bias = turn.tile([P, 32], F32, name="bias", align_bytes=64, offset=0)
+        nc.vector.transpose(bias[:], b_rows[:])
+        y_first = turn.tile([P, HALF], F32, name="y_first", align_bytes=64, offset=512)
+        for lo in (0, PIECE):
+            acc = psum.tile([P, PIECE], F32, name="acc")
+            multiply(0, acc[:], lo, lo + PIECE)
+            nc.scalar.activation(y_first[:, lo : lo + PIECE], acc[:], IDENTITY, bias=bias[:, 0:1])
+        scatter(0, 0, HALF, y_first)
+        for c in range(1, 3):
+            place(c, 0, HALF)
+        rest = turn.tile([P, HALF, 4], BF16, name="rest", align_bytes=64, offset=512)
+        cast(rest, 1, 0, 0, HALF, nc.scalar.copy)
+        quantize(rest, HALF, S)
+        place(3, 0, HALF, turn.tile([P, HALF], F32, name="y_late", align_bytes=64, offset=2048))
+        for c in range(3 + 1, SPLIT):
+            place(c, 0, HALF)
+        for c in range(SPLIT):
+            place(c, HALF, S)
+        for c in range(SPLIT, BLOCKS):
             place(c, 0, S)

@@ -12,7 +12,7 @@ HALF = 128
 PIECE = 64
 SPLIT = 5
 WINDOWS = 5
-W_CUTS = (0, 3, 5, 8)
+W_CUTS = (0, 2, 4, 8)
 F32 = mybir.dt.float32
 BF16 = mybir.dt.bfloat16
 I32 = mybir.dt.int32
@@ -70,17 +70,17 @@ def tile_list_hscat_bias_kernel(tc, x, w_words, w_scales, b, wgo, offs, out):
         nc.gpsimd.memset(b_rows[:], 0.0)
         load_scales(0, nc.sync)
         load_x(0, nc.scalar)
-        load_scales(1, nc.sync)
-        load_w(0, nc.scalar)
-        load_scales(2, nc.sync)
-        load_wgo(0, nc.scalar)
-        load_scales(3, nc.sync)
         load_b(nc.sync)
+        load_scales(1, nc.scalar)
+        load_scales(2, nc.sync)
+        load_w(0, nc.scalar)
+        load_scales(3, nc.sync)
+        load_wgo(0, nc.scalar)
         nc.sync.dma_start(offsets[:], offs)
-        load_x(1, nc.sync)
         load_w(1, nc.sync)
-        load_wgo(1, nc.sync)
+        load_x(1, nc.sync)
         load_w(2, nc.sync)
+        load_wgo(1, nc.sync)
 
         for window in windows[0:4]:
             nc.vector.memset(window[:], 0.0)
@@ -135,15 +135,15 @@ def tile_list_hscat_bias_kernel(tc, x, w_words, w_scales, b, wgo, offs, out):
                 else:
                     nc.sync.dma_start(out[n : n + P, :], window[:])
 
+        bias = keep.tile([P, 32], F32, name="bias", align_bytes=64)
+        nc.vector.transpose(bias[:], b_rows[:])
         piece0 = keep.tile([P, PIECE, 4], BF16, name="piece0", align_bytes=64)
-        piece1 = turn.tile([P, PIECE, 4], BF16, name="piece1", align_bytes=64, offset=0)
+        piece1 = keep.tile([P, PIECE, 4], BF16, name="piece1", align_bytes=64)
         cast(piece0, 0, 0, 0, PIECE, nc.vector.tensor_copy)
         cast(piece1, 0, PIECE, 0, 32, nc.vector.tensor_copy)
         cast(piece1, 0, PIECE, 32, PIECE, nc.scalar.copy)
         quantize(piece0, 0, PIECE)
         quantize(piece1, PIECE, HALF)
-        bias = turn.tile([P, 32], F32, name="bias", align_bytes=64, offset=0)
-        nc.vector.transpose(bias[:], b_rows[:])
         y_first = turn.tile([P, HALF], F32, name="y_first", align_bytes=64, offset=512)
         for lo in (0, PIECE):
             acc = psum.tile([P, PIECE], F32, name="acc")

@@ -10,8 +10,8 @@ P = 128
 BLOCKS = M // P
 HALF = 128
 PIECE = 64
-SPLIT = 5
-WINDOWS = 5
+SPLIT = 6
+WINDOWS = 6
 W_CUTS = (0, 2, 4, 8)
 F32 = mybir.dt.float32
 BF16 = mybir.dt.bfloat16
@@ -36,7 +36,7 @@ def tile_list_hscat_bias_kernel(tc, x, w_words, w_scales, b, wgo, offs, out):
         xv = x.rearrange("(p j) w -> p j w", j=4)
         raw = [
             keep.tile([P, 4, HALF], F32, name="raw0"),
-            turn.tile([P, 4, HALF], F32, name="raw1", align_bytes=64, offset=2048),
+            turn.tile([P, 4, HALF], F32, name="raw1", align_bytes=64, offset=6144),
         ]
         w_bytes = w_words[0].rearrange("p n t -> p (n t)")
         w_parts = [
@@ -46,7 +46,7 @@ def tile_list_hscat_bias_kernel(tc, x, w_words, w_scales, b, wgo, offs, out):
         w_sc = keep.tile([P, M // 4], U8, name="w_sc", align_bytes=64)
         wgo_sb = keep.tile([P, S], F32, name="wgo_sb")
         b_rows = keep.tile([P, 32], F32, name="b_rows", align_bytes=64)
-        windows = [keep.tile([P, T], F32, name=f"window{i}") for i in range(WINDOWS)]
+        windows = [keep.tile([P, T], F32, name=f"window{i}") for i in range(4)]
 
         def load_scales(q, engine):
             engine.dma_start(
@@ -82,10 +82,8 @@ def tile_list_hscat_bias_kernel(tc, x, w_words, w_scales, b, wgo, offs, out):
         load_w(2, nc.sync)
         load_wgo(1, nc.sync)
 
-        for window in windows[0:4]:
+        for window in windows:
             nc.vector.memset(window[:], 0.0)
-        for window in windows[4:]:
-            nc.gpsimd.memset(window[:], 0.0)
 
         codes = keep.tile([P, S], U32, name="codes", align_bytes=64)
         scales = keep.tile([P, S], U8, name="scales", align_bytes=64)
@@ -138,25 +136,28 @@ def tile_list_hscat_bias_kernel(tc, x, w_words, w_scales, b, wgo, offs, out):
         bias = keep.tile([P, 32], F32, name="bias", align_bytes=64)
         nc.vector.transpose(bias[:], b_rows[:])
         piece0 = keep.tile([P, PIECE, 4], BF16, name="piece0", align_bytes=64)
-        piece1 = keep.tile([P, PIECE, 4], BF16, name="piece1", align_bytes=64)
+        piece1 = turn.tile([P, PIECE, 4], BF16, name="piece1", align_bytes=64, offset=1792)
         cast(piece0, 0, 0, 0, PIECE, nc.vector.tensor_copy)
         cast(piece1, 0, PIECE, 0, 32, nc.vector.tensor_copy)
         cast(piece1, 0, PIECE, 32, PIECE, nc.scalar.copy)
         quantize(piece0, 0, PIECE)
         quantize(piece1, PIECE, HALF)
-        y_first = turn.tile([P, HALF], F32, name="y_first", align_bytes=64, offset=512)
+        for i in range(4, WINDOWS):
+            windows.append(turn.tile([P, T], F32, name=f"window{i}", align_bytes=64, offset=2048 * (i - 4)))
+            nc.gpsimd.memset(windows[i][:], 0.0)
+        y_first = turn.tile([P, HALF], F32, name="y_first", align_bytes=64, offset=4096)
         for lo in (0, PIECE):
             acc = psum.tile([P, PIECE], F32, name="acc")
             multiply(0, acc[:], lo, lo + PIECE)
             nc.scalar.activation(y_first[:, lo : lo + PIECE], acc[:], IDENTITY, bias=bias[:, 0:1])
         scatter(0, 0, HALF, y_first)
-        for c in range(1, 3):
+        for c in range(1, 4):
             place(c, 0, HALF)
-        rest = turn.tile([P, HALF, 4], BF16, name="rest", align_bytes=64, offset=512)
+        rest = turn.tile([P, HALF, 4], BF16, name="rest", align_bytes=64, offset=4096)
         cast(rest, 1, 0, 0, HALF, nc.scalar.copy)
         quantize(rest, HALF, S)
-        place(3, 0, HALF, turn.tile([P, HALF], F32, name="y_late", align_bytes=64, offset=2048))
-        for c in range(3 + 1, SPLIT):
+        place(4, 0, HALF, turn.tile([P, HALF], F32, name="y_late", align_bytes=64, offset=6144))
+        for c in range(4 + 1, SPLIT):
             place(c, 0, HALF)
         for c in range(SPLIT):
             place(c, HALF, S)

@@ -35,7 +35,7 @@ def tile_list_hscat_bias_kernel(tc, x, w_words, w_scales, b, wgo, offs, out):
         offsets = keep.tile([P, S // 16], U16, name="offsets")
         xv = x.rearrange("(p j) w -> p j w", j=4)
         raw = [
-            keep.tile([P, 4, HALF], F32, name="raw0"),
+            turn.tile([P, 4, HALF], F32, name="raw0", align_bytes=64, offset=8192),
             turn.tile([P, 4, HALF], F32, name="raw1", align_bytes=64, offset=6144),
         ]
         w_bytes = w_words[0].rearrange("p n t -> p (n t)")
@@ -133,8 +133,6 @@ def tile_list_hscat_bias_kernel(tc, x, w_words, w_scales, b, wgo, offs, out):
                 else:
                     nc.sync.dma_start(out[n : n + P, :], window[:])
 
-        bias = keep.tile([P, 32], F32, name="bias", align_bytes=64)
-        nc.vector.transpose(bias[:], b_rows[:])
         piece0 = keep.tile([P, PIECE, 4], BF16, name="piece0", align_bytes=64)
         piece1 = turn.tile([P, PIECE, 4], BF16, name="piece1", align_bytes=64, offset=1792)
         cast(piece0, 0, 0, 0, PIECE, nc.vector.tensor_copy)
@@ -142,6 +140,8 @@ def tile_list_hscat_bias_kernel(tc, x, w_words, w_scales, b, wgo, offs, out):
         cast(piece1, 0, PIECE, 32, PIECE, nc.scalar.copy)
         quantize(piece0, 0, PIECE)
         quantize(piece1, PIECE, HALF)
+        bias = turn.tile([P, 32], F32, name="bias", align_bytes=64, offset=8192)
+        nc.vector.transpose(bias[:], b_rows[:])
         for i in range(4, WINDOWS):
             windows.append(turn.tile([P, T], F32, name=f"window{i}", align_bytes=64, offset=2048 * (i - 4)))
             nc.gpsimd.memset(windows[i][:], 0.0)

@@ -70,12 +70,12 @@ def tile_list_hscat_bias_kernel(tc, x, w_words, w_scales, b, wgo, offs, out):
         nc.gpsimd.memset(b_rows[:], 0.0)
         load_scales(0, nc.sync)
         load_x(0, nc.scalar)
-        load_b(nc.sync)
-        load_scales(1, nc.scalar)
-        load_scales(2, nc.sync)
+        load_scales(1, nc.sync)
         load_w(0, nc.scalar)
-        load_scales(3, nc.sync)
+        load_scales(2, nc.sync)
         load_wgo(0, nc.scalar)
+        load_scales(3, nc.sync)
+        load_b(nc.sync)
         nc.sync.dma_start(offsets[:], offs)
         load_w(1, nc.sync)
         load_x(1, nc.sync)

@@ -127,7 +127,7 @@ def tile_list_hscat_bias_kernel(tc, x, w_words, w_scales, b, wgo, offs, out):
             window = windows[c % WINDOWS]
             nc.vector.tensor_tensor(window[:].indirect(offsets[:, lo // 16 : hi // 16]), y[:], wgo_sb[:, lo:hi], MULT)
             if hi == S:
-                if 4 <= c < BLOCKS - 1:
+                if 2 <= c < 5:
                     nc.sync.dma_start(out[n : n + P, 0 : T // 2], window[:, 0 : T // 2])
                     nc.sync.dma_start(out[n : n + P, T // 2 : T], window[:, T // 2 : T])
                 else:

@@ -10,8 +10,8 @@ P = 128
 BLOCKS = M // P
 HALF = 128
 PIECE = 64
-SPLIT = 6
-WINDOWS = 6
+SPLIT = 8
+WINDOWS = 8
 W_CUTS = (0, 2, 4, 8)
 F32 = mybir.dt.float32
 BF16 = mybir.dt.bfloat16
@@ -46,7 +46,7 @@ def tile_list_hscat_bias_kernel(tc, x, w_words, w_scales, b, wgo, offs, out):
         w_sc = keep.tile([P, M // 4], U8, name="w_sc", align_bytes=64)
         wgo_sb = keep.tile([P, S], F32, name="wgo_sb")
         b_rows = keep.tile([P, 32], F32, name="b_rows", align_bytes=64)
-        windows = [keep.tile([P, T], F32, name=f"window{i}") for i in range(4)]
+        windows = [keep.tile([P, T], F32, name=f"window{i}") for i in range(6)]
 
         def load_scales(q, engine):
             engine.dma_start(
@@ -142,8 +142,8 @@ def tile_list_hscat_bias_kernel(tc, x, w_words, w_scales, b, wgo, offs, out):
         quantize(piece1, PIECE, HALF)
         bias = turn.tile([P, 32], F32, name="bias", align_bytes=64, offset=8192)
         nc.vector.transpose(bias[:], b_rows[:])
-        for i in range(4, WINDOWS):
-            windows.append(turn.tile([P, T], F32, name=f"window{i}", align_bytes=64, offset=2048 * (i - 4)))
+        for i in range(6, WINDOWS):
+            windows.append(turn.tile([P, T], F32, name=f"window{i}", align_bytes=64, offset=2048 * (i - 6)))
             nc.gpsimd.memset(windows[i][:], 0.0)
         y_first = turn.tile([P, HALF], F32, name="y_first", align_bytes=64, offset=4096)
         for lo in (0, PIECE):
@@ -161,5 +161,3 @@ def tile_list_hscat_bias_kernel(tc, x, w_words, w_scales, b, wgo, offs, out):
             place(c, 0, HALF)
         for c in range(SPLIT):
             place(c, HALF, S)
-        for c in range(SPLIT, BLOCKS):
-            place(c, 0, S)

from contextlib import ExitStack

import concourse.mybir as mybir


K, M, T, S = 512, 1024, 512, 256
FLOPS = 2 * K * M * S

P = 128
BLOCKS = M // P
HALF = 128
PIECE = 64
SPLIT = 8
WINDOWS = 8
W_CUTS = (0, 2, 4, 8)
F32 = mybir.dt.float32
BF16 = mybir.dt.bfloat16
I32 = mybir.dt.int32
U32 = mybir.dt.uint32
U16 = mybir.dt.uint16
U8 = mybir.dt.uint8
FP8X4 = mybir.dt.float8_e4m3fn_x4
MULT = mybir.AluOpType.mult
IDENTITY = mybir.ActivationFunctionType.Identity


def tile_list_hscat_bias_kernel(tc, x, w_words, w_scales, b, wgo, offs, out):
    nc = tc.nc
    with ExitStack() as ctx:
        keep = ctx.enter_context(tc.tile_pool(name="keep", bufs=1))
        turn = ctx.enter_context(tc.tile_pool(name="turn", bufs=1))
        ypool = ctx.enter_context(tc.tile_pool(name="ypool", bufs=8))
        psum = ctx.enter_context(tc.psum_pool(name="psum", bufs=8))

        offsets = keep.tile([P, S // 16], U16, name="offsets")
        xv = x.rearrange("(p j) w -> p j w", j=4)
        raw = [
            turn.tile([P, 4, HALF], F32, name="raw0", align_bytes=64, offset=8192),
            turn.tile([P, 4, HALF], F32, name="raw1", align_bytes=64, offset=6144),
        ]
        w_bytes = w_words[0].rearrange("p n t -> p (n t)")
        w_parts = [
            keep.tile([P, P * (W_CUTS[i + 1] - W_CUTS[i])], U32, name=f"w_part{i}", align_bytes=64)
            for i in range(len(W_CUTS) - 1)
        ]
        w_sc = keep.tile([P, M // 4], U8, name="w_sc", align_bytes=64)
        wgo_sb = keep.tile([P, S], F32, name="wgo_sb")
        b_rows = keep.tile([P, 32], F32, name="b_rows", align_bytes=64)
        windows = [keep.tile([P, T], F32, name=f"window{i}") for i in range(6)]

        def load_scales(q, engine):
            engine.dma_start(
                w_sc[32 * q : 32 * q + 16, :].bitcast(I32),
                w_scales[0][4 * q : 4 * q + 4, :].rearrange("r (a n) -> a r n", a=4).bitcast(I32),
            )

        def load_x(h, engine):
            engine.dma_start(raw[h][:], xv[:, :, HALF * h : HALF * (h + 1)])

        def load_w(i, engine):
            lo, hi = 4 * P * W_CUTS[i], 4 * P * W_CUTS[i + 1]
            engine.dma_start(w_parts[i][:].bitcast(I32), w_bytes[:, lo:hi].bitcast(I32))

        def load_wgo(h, engine):
            engine.dma_start(wgo_sb[:, HALF * h : HALF * (h + 1)], wgo[:, HALF * h : HALF * (h + 1)])

        def load_b(engine):
            engine.dma_start(b_rows[0:P:4, :], b.rearrange("(c q i) -> q c i", q=4, i=32))

        nc.gpsimd.memset(b_rows[:], 0.0)
        load_scales(0, nc.sync)
        load_x(0, nc.scalar)
        load_scales(1, nc.sync)
        load_w(0, nc.scalar)
        load_scales(2, nc.sync)
        load_wgo(0, nc.scalar)
        load_scales(3, nc.sync)
        load_b(nc.sync)
        nc.sync.dma_start(offsets[:], offs)
        load_w(1, nc.sync)
        load_x(1, nc.sync)
        load_w(2, nc.sync)
        load_wgo(1, nc.sync)

        for window in windows:
            nc.vector.memset(window[:], 0.0)

        codes = keep.tile([P, S], U32, name="codes", align_bytes=64)
        scales = keep.tile([P, S], U8, name="scales", align_bytes=64)

        def cast(piece, h, base, lo, hi, engine_copy):
            engine_copy(
                piece[:, lo:hi, :].rearrange("p (c i) t -> p c t i", i=4),
                raw[h][:, :, base + lo : base + hi].rearrange("p t (c i) -> p c t i", i=4),
            )

        def quantize(piece, lo, hi):
            nc.vector.quantize_mx(
                out=codes[:, lo:hi].bitcast(FP8X4),
                scales=scales[:, lo:hi],
                in_=piece[:].rearrange("p w t -> p (w t)"),
            )

        def multiply(c, acc, lo, hi):
            i = max(k for k in range(len(W_CUTS) - 1) if W_CUTS[k] <= c)
            first = P * (c - W_CUTS[i])
            nc.tensor.matmul_mx(
                out=acc,
                lhsT=w_parts[i][:, first : first + P].bitcast(FP8X4),
                lhsT_scale=w_sc[4 * (c // 2) :, P * (c % 2) : P * (c % 2 + 1)],
                rhs=codes[:, lo:hi].bitcast(FP8X4),
                rhs_scale=scales[:, lo:hi],
                start=True,
                stop=True,
            )

        def place(c, lo, hi, y=None):
            acc = psum.tile([P, hi - lo], F32, name="acc")
            multiply(c, acc[:], lo, hi)
            if y is None:
                y = ypool.tile([P, hi - lo], F32, name="y")
            nc.scalar.activation(y[:], acc[:], IDENTITY, bias=bias[:, 4 * c : 4 * c + 1])
            scatter(c, lo, hi, y)

        def scatter(c, lo, hi, y):
            n = P * c
            window = windows[c % WINDOWS]
            nc.vector.tensor_tensor(window[:].indirect(offsets[:, lo // 16 : hi // 16]), y[:], wgo_sb[:, lo:hi], MULT)
            if hi == S:
                if 2 <= c < 5:
                    nc.sync.dma_start(out[n : n + P, 0 : T // 2], window[:, 0 : T // 2])
                    nc.sync.dma_start(out[n : n + P, T // 2 : T], window[:, T // 2 : T])
                else:
                    nc.sync.dma_start(out[n : n + P, :], window[:])

        piece0 = keep.tile([P, PIECE, 4], BF16, name="piece0", align_bytes=64)
        piece1 = turn.tile([P, PIECE, 4], BF16, name="piece1", align_bytes=64, offset=1792)
        cast(piece0, 0, 0, 0, PIECE, nc.vector.tensor_copy)
        cast(piece1, 0, PIECE, 0, 32, nc.vector.tensor_copy)
        cast(piece1, 0, PIECE, 32, PIECE, nc.scalar.copy)
        quantize(piece0, 0, PIECE)
        quantize(piece1, PIECE, HALF)
        bias = turn.tile([P, 32], F32, name="bias", align_bytes=64, offset=8192)
        nc.vector.transpose(bias[:], b_rows[:])
        for i in range(6, WINDOWS):
            windows.append(turn.tile([P, T], F32, name=f"window{i}", align_bytes=64, offset=2048 * (i - 6)))
            nc.gpsimd.memset(windows[i][:], 0.0)
        y_first = turn.tile([P, HALF], F32, name="y_first", align_bytes=64, offset=4096)
        for lo in (0, PIECE):
            acc = psum.tile([P, PIECE], F32, name="acc")
            multiply(0, acc[:], lo, lo + PIECE)
            nc.scalar.activation(y_first[:, lo : lo + PIECE], acc[:], IDENTITY, bias=bias[:, 0:1])
        scatter(0, 0, HALF, y_first)
        for c in range(1, 4):
            place(c, 0, HALF)
        rest = turn.tile([P, HALF, 4], BF16, name="rest", align_bytes=64, offset=4096)
        cast(rest, 1, 0, 0, HALF, nc.scalar.copy)
        quantize(rest, HALF, S)
        place(4, 0, HALF, turn.tile([P, HALF], F32, name="y_late", align_bytes=64, offset=6144))
        for c in range(4 + 1, SPLIT):
            place(c, 0, HALF)
        for c in range(SPLIT):
            place(c, HALF, S)
